import numpy as np
import ml_dtypes


def mxq(x, axis, fmt="e4m3"):
    dtype, down = {"e4m3": (ml_dtypes.float8_e4m3fn, 7), "e5m2": (ml_dtypes.float8_e5m2, 14)}[fmt]
    v = np.moveaxis(np.asarray(x, np.float32).astype(ml_dtypes.bfloat16).astype(np.float64), axis, -1)
    blocks = v.reshape(v.shape[:-1] + (-1, 32))
    amax = np.abs(blocks).max(-1, keepdims=True)
    byte = np.maximum(np.where(amax > 0, np.frexp(amax)[1] - 1 + 127, 0) - down, 1)
    scale = np.exp2(byte - 127.0)
    codes = (blocks / scale).astype(np.float32).astype(dtype).astype(np.float64)
    return np.moveaxis((codes * scale).reshape(v.shape), -1, axis)


WIDE = False


def mx_kscale(k):
    if not WIDE:
        return np.ones(k)
    levels = np.array([10, -10, 5, -5, 0])
    if k % 512:
        return np.exp2(np.random.permutation(np.resize(levels, k // 32))).repeat(32)
    a = np.empty((k // 512, 16))
    for p in range(k // 512):
        a[p, :8] = np.random.permutation(np.resize(levels, 8))
        for g in range(8):
            far = levels[np.abs(levels - a[p, g]) >= 10]
            a[p, g + 8] = far[np.random.randint(len(far))]
    return np.exp2(a.ravel()).repeat(32)


def f64(x):
    return np.asarray(x).astype(np.float64)


def striped8(idx):
    return np.concatenate([v.reshape(-1, 16).T for v in idx]).astype(np.uint16)


def unstriped8(offs):
    return np.stack([offs[16 * g:16 * g + 16].T.reshape(-1) for g in range(8)]).astype(np.int64)


E2M1 = np.array([0.0, 0.5, 1.0, 1.5, 2.0, 3.0, 4.0, 6.0, -0.0, -0.5, -1.0, -1.5, -2.0, -3.0, -4.0, -6.0])


def pack_weight(w, fmt):
    k, n = w.shape
    w = f64(np.asarray(w, np.float32).astype(ml_dtypes.bfloat16)).reshape(k // 32, 32, n)
    amax = np.abs(w).max(1)
    if fmt == "e4m3":
        byte = np.frexp(amax)[1] - 1 + 127 - 7
    else:
        mant, ex = np.frexp(amax / 6.0)
        byte = np.where(mant > 0.5, ex, ex - 1) + 127
    byte = np.clip(np.where(amax > 0, byte, 1), 1, 254)
    scaled = (w * np.exp2(127.0 - byte)[:, None, :]).reshape(k, n).astype(np.float32)
    by_word = np.ascontiguousarray(scaled.reshape(k // 512, 128, 4, n).transpose(0, 1, 3, 2))
    if fmt == "e4m3":
        words = by_word.astype(ml_dtypes.float8_e4m3fn).view(np.uint8)
    else:
        c = by_word.astype(ml_dtypes.float4_e2m1fn).view(np.uint8) & 0xF
        words = (c[..., 0::2] | (c[..., 1::2] << 4)).reshape(k // 512, 128, 2 * n)
    return np.ascontiguousarray(words), np.ascontiguousarray(byte.astype(np.uint8).reshape(k // 512, 16, n))


def unpack_weight(words, scales, fmt):
    g, _, n = scales.shape
    words = np.ascontiguousarray(words).reshape(g, 128, n, -1)
    if fmt == "e4m3":
        vals = words.view(ml_dtypes.float8_e4m3fn).astype(np.float64)
    else:
        nib = np.empty((g, 128, n, 4), np.uint8)
        nib[..., 0::2] = words & 0xF
        nib[..., 1::2] = words >> 4
        vals = E2M1[nib]
    vals = vals * np.repeat(np.exp2(scales.astype(np.float64) - 127.0), 8, axis=1)[..., None]
    return vals.transpose(0, 1, 3, 2).reshape(g * 512, n)


K, M, T, S = 1024, 128, 2048, 1024


def setup_inputs():
    n = np.random.standard_normal
    s = mx_kscale(K)[:, None]
    p_w = pack_weight(n((K, M)) / np.sqrt(K) / s, "e4m3")
    return {
        "x": (n((K, S)) * s).astype(np.float32),
        "w_words": p_w[0],
        "w_scales": p_w[1],
        "b": (0.3 * n(128)).astype(np.float32),
        "wgo": np.repeat(np.random.uniform(0.5, 2.0, (8, S)), 16, axis=0).astype(np.float32),
        "offs": striped8(np.stack([np.random.permutation(T)[:S] for _ in range(8)])),
    }


def reference(x, w_words, w_scales, b, wgo, offs):
    x_ = mxq(f64(x), 0, "e4m3")
    w_ = unpack_weight(w_words, w_scales, "e4m3")
    y = w_.T @ x_
    place = unstriped8(offs)[np.arange(M) % 128 // 16]
    out = np.zeros((M, T))
    out[np.arange(M)[:, None], place] = f64(wgo)[np.arange(M) % 128] * (y + f64(b)[:, None])
    return out

@@ -1,0 +1,132 @@
+from contextlib import ExitStack
+
+import concourse.mybir as mybir
+
+K, M, T, S = 1024, 128, 2048, 1024
+FLOPS = 2 * K * M * S
+
+F32 = mybir.dt.float32
+BF16 = mybir.dt.bfloat16
+I32 = mybir.dt.int32
+U32 = mybir.dt.uint32
+U16 = mybir.dt.uint16
+U8 = mybir.dt.uint8
+FP8X4 = mybir.dt.float8_e4m3fn_x4
+IDENT = mybir.ActivationFunctionType.Identity
+MULT = mybir.AluOpType.mult
+ADD = mybir.AluOpType.add
+
+P = 128
+J = 4
+PASS = P * J
+A = K // PASS
+HALF = 512
+H = S // HALF
+V_COLS = {(0, 0): 352, (0, 1): 352, (1, 0): 0, (1, 1): 320}
+GROUPS = {0: (256, 256), 1: (256, 128, 128)}
+
+
+def tile_list_hscat_bias_kernel(tc, x, w_words, w_scales, b, wgo, offs, out):
+    nc = tc.nc
+    with ExitStack() as ctx:
+        keep = ctx.enter_context(tc.tile_pool(name="keep", bufs=1))
+        psum = ctx.enter_context(tc.psum_pool(name="psum", bufs=1))
+
+        raw = {}
+        for h in range(H):
+            for a in range(A):
+                raw[h, a] = keep.tile([P, J, HALF], F32, name="raw%d%d" % (h, a))
+
+        def load_x(h, a):
+            nc.sync.dma_start(
+                out=raw[h, a][:],
+                in_=x[a * PASS:(a + 1) * PASS, h * HALF:(h + 1) * HALF].rearrange("(p j) w -> p j w", j=J),
+            )
+
+        w_codes = keep.tile([P, A, M], I32, name="w_codes", align_bytes=64)
+        w_sc = keep.tile([P, A, M], U8, name="w_sc", align_bytes=64)
+        bias = keep.tile([P, 1], F32, name="bias")
+        lists = keep.tile([P, S // 16], U16, name="lists")
+        wg = keep.tile([P, S], F32, name="wg")
+        window = keep.tile([P, T], F32, name="window")
+        dummy = keep.tile([P, 1], F32, name="dummy")
+
+        nc.vector.memset(w_sc[:].rearrange("p a n -> p (a n)").bitcast(I32), 0)
+        nc.vector.memset(dummy[:], 0.0)
+        nc.scalar.dma_start(out=w_codes[:], in_=w_words.rearrange("a p n t -> p a (n t)").bitcast(I32))
+        nc.scalar.dma_start(out=bias[:], in_=b.rearrange("(p o) -> p o", o=1))
+        for q in range(4):
+            nc.scalar.dma_start(
+                out=w_sc[32 * q:32 * q + 4, :, :].bitcast(I32),
+                in_=w_scales[:, 4 * q:4 * q + 4, :].rearrange("a r n -> r a n").bitcast(I32),
+            )
+        load_x(0, 0)
+        load_x(0, 1)
+        nc.sync.dma_start(lists[:], offs)
+        nc.sync.dma_start(out=wg[:, 0:HALF], in_=wgo[:, 0:HALF])
+        load_x(1, 0)
+        load_x(1, 1)
+        nc.sync.dma_start(out=wg[:, HALF:S], in_=wgo[:, HALF:S])
+        nc.scalar.activation(dummy[:], dummy[:], IDENT)
+        nc.vector.memset(window[:], 0.0)
+
+        acc = {}
+        for h in range(H):
+            for s in range(len(GROUPS[h])):
+                acc[h, s] = psum.tile([M, GROUPS[h][s]], F32, name="acc%d%d" % (h, s))
+
+        for h in range(H):
+            y = keep.tile([M, HALF], F32, name="y%d" % h)
+            for a in range(A):
+                grouped = keep.tile([P, HALF, J], BF16, name="grouped%d%d" % (h, a), align_bytes=64)
+                codes = keep.tile([P, HALF], U32, name="codes%d%d" % (h, a), align_bytes=64)
+                scales = keep.tile([P, HALF], U8, name="scales%d%d" % (h, a), align_bytes=64)
+
+                def views(c0, c1):
+                    return (
+                        grouped[:, c0:c1, :].rearrange("p (c i) t -> p c t i", i=4),
+                        raw[h, a][:, :, c0:c1].rearrange("p t (c i) -> p c t i", i=4),
+                    )
+
+                vc = V_COLS[h, a]
+                if vc > 0:
+                    dst, src = views(0, vc)
+                    nc.vector.tensor_copy(out=dst, in_=src)
+                if vc < 256:
+                    dst, src = views(vc, 256)
+                    nc.scalar.copy(dst, src)
+                dst, src = views(max(vc, 256), HALF)
+                nc.scalar.copy(dst, src)
+                c0 = 0
+                for s in range(len(GROUPS[h])):
+                    cols = slice(c0, c0 + GROUPS[h][s])
+                    c0 += GROUPS[h][s]
+                    nc.vector.quantize_mx(
+                        out=codes[:, cols].bitcast(FP8X4),
+                        scales=scales[:, cols],
+                        in_=grouped[:, cols, :].rearrange("p w j -> p (w j)"),
+                    )
+                    nc.tensor.matmul_mx(
+                        out=acc[h, s][:],
+                        lhsT=w_codes[:, a, :].bitcast(FP8X4),
+                        lhsT_scale=w_sc[:, a, :],
+                        rhs=codes[:, cols].bitcast(FP8X4),
+                        rhs_scale=scales[:, cols],
+                        start=(a == 0),
+                        stop=(a == A - 1),
+                    )
+            c0 = 0
+            for s in range(len(GROUPS[h])):
+                cols = slice(c0, c0 + GROUPS[h][s])
+                c0 += GROUPS[h][s]
+                if s == len(GROUPS[h]) - 1:
+                    nc.vector.tensor_scalar(out=y[:, cols], in0=acc[h, s][:], scalar1=bias[:], scalar2=None, op0=ADD)
+                else:
+                    nc.scalar.activation(y[:, cols], acc[h, s][:], IDENT, bias=bias[:])
+            nc.vector.tensor_tensor(
+                window[:].indirect(lists[:, h * HALF // 16:(h + 1) * HALF // 16]),
+                y[:],
+                wg[:, h * HALF:(h + 1) * HALF],
+                MULT,
+            )
+        nc.sync.dma_start(out=out, in_=window[:])

@@ -14,7 +14,6 @@ U8 = mybir.dt.uint8
 FP8X4 = mybir.dt.float8_e4m3fn_x4
 IDENT = mybir.ActivationFunctionType.Identity
 MULT = mybir.AluOpType.mult
-ADD = mybir.AluOpType.add
 
 P = 128
 J = 4
@@ -22,8 +21,7 @@ PASS = P * J
 A = K // PASS
 HALF = 512
 H = S // HALF
-V_COLS = {(0, 0): 352, (0, 1): 352, (1, 0): 0, (1, 1): 320}
-GROUPS = {0: (256, 256), 1: (256, 128, 128)}
+EDGES = (0, 256, 384, 512)
 
 
 def tile_list_hscat_bias_kernel(tc, x, w_words, w_scales, b, wgo, offs, out):
@@ -32,101 +30,134 @@ def tile_list_hscat_bias_kernel(tc, x, w_words, w_scales, b, wgo, offs, out):
         keep = ctx.enter_context(tc.tile_pool(name="keep", bufs=1))
         psum = ctx.enter_context(tc.psum_pool(name="psum", bufs=1))
 
-        raw = {}
+        chunks = keep.tile([P, H * A, J, HALF], F32, name="chunks")
+        raw, grouped, codes, scales = {}, {}, {}, {}
         for h in range(H):
             for a in range(A):
-                raw[h, a] = keep.tile([P, J, HALF], F32, name="raw%d%d" % (h, a))
+                raw[h, a] = chunks[:, h * A + a]
+                grouped[h, a] = keep.tile([P, HALF, J], BF16, name="grouped%d%d" % (h, a), align_bytes=64)
+                codes[h, a] = keep.tile([P, HALF], U32, name="codes%d%d" % (h, a), align_bytes=64)
+                scales[h, a] = keep.tile([P, HALF], U8, name="scales%d%d" % (h, a), align_bytes=64)
 
-        def load_x(h, a):
+        def load_x(h, a, c0=0, c1=HALF):
             nc.sync.dma_start(
-                out=raw[h, a][:],
-                in_=x[a * PASS:(a + 1) * PASS, h * HALF:(h + 1) * HALF].rearrange("(p j) w -> p j w", j=J),
+                out=raw[h, a][:, :, c0:c1],
+                in_=x[a * PASS:(a + 1) * PASS, h * HALF + c0:h * HALF + c1].rearrange("(p j) w -> p j w", j=J),
             )
 
         w_codes = keep.tile([P, A, M], I32, name="w_codes", align_bytes=64)
         w_sc = keep.tile([P, A, M], U8, name="w_sc", align_bytes=64)
         bias = keep.tile([P, 1], F32, name="bias")
         lists = keep.tile([P, S // 16], U16, name="lists")
-        wg = keep.tile([P, S], F32, name="wg")
+        wg = {}
+        for h in range(H):
+            wg[h] = keep.tile([P, HALF], F32, name="wg%d" % h)
         window = keep.tile([P, T], F32, name="window")
         dummy = keep.tile([P, 1], F32, name="dummy")
 
         nc.vector.memset(w_sc[:].rearrange("p a n -> p (a n)").bitcast(I32), 0)
+        nc.vector.memset(chunks[:, 1:, 0, 0:1], 0.0)
+        nc.vector.memset(w_codes[:, 0, 0:1], 0)
+        nc.vector.memset(wg[0][:, 0:1], 0.0)
         nc.vector.memset(dummy[:], 0.0)
-        nc.scalar.dma_start(out=w_codes[:], in_=w_words.rearrange("a p n t -> p a (n t)").bitcast(I32))
-        nc.scalar.dma_start(out=bias[:], in_=b.rearrange("(p o) -> p o", o=1))
+        nc.gpsimd.dma_start(out=bias[:], in_=b.rearrange("(p o) -> p o", o=1))
+        load_x(0, 0)
         for q in range(4):
-            nc.scalar.dma_start(
+            nc.sync.dma_start(
                 out=w_sc[32 * q:32 * q + 4, :, :].bitcast(I32),
                 in_=w_scales[:, 4 * q:4 * q + 4, :].rearrange("a r n -> r a n").bitcast(I32),
             )
-        load_x(0, 0)
         load_x(0, 1)
+        nc.sync.dma_start(out=w_codes[:], in_=w_words.rearrange("a p n t -> p a (n t)").bitcast(I32))
         nc.sync.dma_start(lists[:], offs)
-        nc.sync.dma_start(out=wg[:, 0:HALF], in_=wgo[:, 0:HALF])
+        nc.sync.dma_start(out=wg[0][:], in_=wgo[:, 0:HALF])
         load_x(1, 0)
         load_x(1, 1)
-        nc.sync.dma_start(out=wg[:, HALF:S], in_=wgo[:, HALF:S])
+        nc.sync.dma_start(out=wg[1][:], in_=wgo[:, HALF:S])
         nc.scalar.activation(dummy[:], dummy[:], IDENT)
         nc.vector.memset(window[:], 0.0)
 
-        acc = {}
+        y, acc = {}, {}
         for h in range(H):
-            for s in range(len(GROUPS[h])):
-                acc[h, s] = psum.tile([M, GROUPS[h][s]], F32, name="acc%d%d" % (h, s))
+            y[h] = keep.tile([M, HALF], F32, name="y%d" % h)
+            for s in range(3):
+                acc[h, s] = psum.tile([M, EDGES[s + 1] - EDGES[s]], F32, name="acc%d%d" % (h, s))
 
-        for h in range(H):
-            y = keep.tile([M, HALF], F32, name="y%d" % h)
-            for a in range(A):
-                grouped = keep.tile([P, HALF, J], BF16, name="grouped%d%d" % (h, a), align_bytes=64)
-                codes = keep.tile([P, HALF], U32, name="codes%d%d" % (h, a), align_bytes=64)
-                scales = keep.tile([P, HALF], U8, name="scales%d%d" % (h, a), align_bytes=64)
+        def interleave(copy, h, a, c0, c1):
+            copy(
+                grouped[h, a][:, c0:c1, :].rearrange("p (c i) t -> p c t i", i=4),
+                raw[h, a][:, :, c0:c1].rearrange("p t (c i) -> p c t i", i=4),
+            )
 
-                def views(c0, c1):
-                    return (
-                        grouped[:, c0:c1, :].rearrange("p (c i) t -> p c t i", i=4),
-                        raw[h, a][:, :, c0:c1].rearrange("p t (c i) -> p c t i", i=4),
-                    )
+        def quantize(h, a, c0, c1):
+            nc.vector.quantize_mx(
+                out=codes[h, a][:, c0:c1].bitcast(FP8X4),
+                scales=scales[h, a][:, c0:c1],
+                in_=grouped[h, a][:, c0:c1, :].rearrange("p w j -> p (w j)"),
+            )
 
-                vc = V_COLS[h, a]
-                if vc > 0:
-                    dst, src = views(0, vc)
-                    nc.vector.tensor_copy(out=dst, in_=src)
-                if vc < 256:
-                    dst, src = views(vc, 256)
-                    nc.scalar.copy(dst, src)
-                dst, src = views(max(vc, 256), HALF)
-                nc.scalar.copy(dst, src)
-                c0 = 0
-                for s in range(len(GROUPS[h])):
-                    cols = slice(c0, c0 + GROUPS[h][s])
-                    c0 += GROUPS[h][s]
-                    nc.vector.quantize_mx(
-                        out=codes[:, cols].bitcast(FP8X4),
-                        scales=scales[:, cols],
-                        in_=grouped[:, cols, :].rearrange("p w j -> p (w j)"),
-                    )
-                    nc.tensor.matmul_mx(
-                        out=acc[h, s][:],
-                        lhsT=w_codes[:, a, :].bitcast(FP8X4),
-                        lhsT_scale=w_sc[:, a, :],
-                        rhs=codes[:, cols].bitcast(FP8X4),
-                        rhs_scale=scales[:, cols],
-                        start=(a == 0),
-                        stop=(a == A - 1),
-                    )
-            c0 = 0
-            for s in range(len(GROUPS[h])):
-                cols = slice(c0, c0 + GROUPS[h][s])
-                c0 += GROUPS[h][s]
-                if s == len(GROUPS[h]) - 1:
-                    nc.vector.tensor_scalar(out=y[:, cols], in0=acc[h, s][:], scalar1=bias[:], scalar2=None, op0=ADD)
-                else:
-                    nc.scalar.activation(y[:, cols], acc[h, s][:], IDENT, bias=bias[:])
+        def multiply(h, a, s):
+            c0, c1 = EDGES[s:s + 2]
+            nc.tensor.matmul_mx(
+                out=acc[h, s][:],
+                lhsT=w_codes[:, a, :].bitcast(FP8X4),
+                lhsT_scale=w_sc[:, a, :],
+                rhs=codes[h, a][:, c0:c1].bitcast(FP8X4),
+                rhs_scale=scales[h, a][:, c0:c1],
+                start=(a == 0),
+                stop=(a == A - 1),
+            )
+
+        def finish(h, s):
+            c0, c1 = EDGES[s:s + 2]
+            nc.scalar.activation(y[h][:, c0:c1], acc[h, s][:], IDENT, bias=bias[:])
+
+        def scatter(h):
             nc.vector.tensor_tensor(
                 window[:].indirect(lists[:, h * HALF // 16:(h + 1) * HALF // 16]),
-                y[:],
-                wg[:, h * HALF:(h + 1) * HALF],
+                y[h][:],
+                wg[h][:],
                 MULT,
             )
+
+        V, SC = nc.vector.tensor_copy, nc.scalar.copy
+        interleave(V, 0, 0, 0, 128)
+        interleave(V, 0, 0, 128, 256)
+        interleave(SC, 0, 0, 256, 512)
+        quantize(0, 0, 0, 512)
+        for s in range(3):
+            multiply(0, 0, s)
+        interleave(V, 0, 1, 0, 128)
+        interleave(V, 0, 1, 128, 256)
+        interleave(SC, 0, 1, 256, 384)
+        interleave(SC, 0, 1, 384, 512)
+        quantize(0, 1, 0, 128)
+        quantize(0, 1, 128, 256)
+        multiply(0, 1, 0)
+        finish(0, 0)
+        quantize(0, 1, 256, 384)
+        multiply(0, 1, 1)
+        finish(0, 1)
+        quantize(0, 1, 384, 512)
+        multiply(0, 1, 2)
+        finish(0, 2)
+        scatter(0)
+        interleave(SC, 1, 0, 0, 256)
+        interleave(SC, 1, 0, 256, 512)
+        interleave(SC, 1, 1, 224, 384)
+        interleave(SC, 1, 1, 384, 512)
+        interleave(V, 1, 1, 0, 224)
+        quantize(1, 0, 0, 512)
+        for s in range(3):
+            multiply(1, 0, s)
+        quantize(1, 1, 0, 256)
+        multiply(1, 1, 0)
+        finish(1, 0)
+        quantize(1, 1, 256, 384)
+        multiply(1, 1, 1)
+        finish(1, 1)
+        quantize(1, 1, 384, 512)
+        multiply(1, 1, 2)
+        finish(1, 2)
+        scatter(1)
         nc.sync.dma_start(out=out, in_=window[:])

@@ -55,20 +55,21 @@ def tile_list_hscat_bias_kernel(tc, x, w_words, w_scales, b, wgo, offs, out):
         window = keep.tile([P, T], F32, name="window")
         dummy = keep.tile([P, 1], F32, name="dummy")
 
+        nc.scalar.dma_start(out=w_codes[:], in_=w_words.rearrange("a p n t -> p a (n t)").bitcast(I32))
         nc.vector.memset(w_sc[:].rearrange("p a n -> p (a n)").bitcast(I32), 0)
-        nc.vector.memset(chunks[:, 1:, 0, 0:1], 0.0)
-        nc.vector.memset(w_codes[:, 0, 0:1], 0)
+        nc.vector.memset(chunks[:, 1:, 0, 0:HALF:256], 0.0)
+        nc.vector.memset(bias[:], 0.0)
         nc.vector.memset(wg[0][:, 0:1], 0.0)
         nc.vector.memset(dummy[:], 0.0)
-        nc.gpsimd.dma_start(out=bias[:], in_=b.rearrange("(p o) -> p o", o=1))
         load_x(0, 0)
         for q in range(4):
             nc.sync.dma_start(
                 out=w_sc[32 * q:32 * q + 4, :, :].bitcast(I32),
                 in_=w_scales[:, 4 * q:4 * q + 4, :].rearrange("a r n -> r a n").bitcast(I32),
             )
-        load_x(0, 1)
-        nc.sync.dma_start(out=w_codes[:], in_=w_words.rearrange("a p n t -> p a (n t)").bitcast(I32))
+        load_x(0, 1, 0, 256)
+        load_x(0, 1, 256, HALF)
+        nc.sync.dma_start(out=bias[:], in_=b.rearrange("(p o) -> p o", o=1))
         nc.sync.dma_start(lists[:], offs)
         nc.sync.dma_start(out=wg[0][:], in_=wgo[:, 0:HALF])
         load_x(1, 0)
@@ -127,14 +128,13 @@ def tile_list_hscat_bias_kernel(tc, x, w_words, w_scales, b, wgo, offs, out):
         quantize(0, 0, 0, 512)
         for s in range(3):
             multiply(0, 0, s)
-        interleave(V, 0, 1, 0, 128)
-        interleave(V, 0, 1, 128, 256)
-        interleave(SC, 0, 1, 256, 384)
-        interleave(SC, 0, 1, 384, 512)
-        quantize(0, 1, 0, 128)
-        quantize(0, 1, 128, 256)
+        interleave(V, 0, 1, 0, 160)
+        interleave(SC, 0, 1, 160, 256)
+        quantize(0, 1, 0, 256)
         multiply(0, 1, 0)
         finish(0, 0)
+        interleave(V, 0, 1, 256, 384)
+        interleave(SC, 0, 1, 384, 512)
         quantize(0, 1, 256, 384)
         multiply(0, 1, 1)
         finish(0, 1)
@@ -144,20 +144,15 @@ def tile_list_hscat_bias_kernel(tc, x, w_words, w_scales, b, wgo, offs, out):
         scatter(0)
         interleave(SC, 1, 0, 0, 256)
         interleave(SC, 1, 0, 256, 512)
-        interleave(SC, 1, 1, 224, 384)
-        interleave(SC, 1, 1, 384, 512)
-        interleave(V, 1, 1, 0, 224)
         quantize(1, 0, 0, 512)
         for s in range(3):
             multiply(1, 0, s)
-        quantize(1, 1, 0, 256)
-        multiply(1, 1, 0)
-        finish(1, 0)
-        quantize(1, 1, 256, 384)
-        multiply(1, 1, 1)
-        finish(1, 1)
-        quantize(1, 1, 384, 512)
-        multiply(1, 1, 2)
-        finish(1, 2)
+        interleave(SC, 1, 1, 384, 512)
+        interleave(V, 1, 1, 0, 256)
+        interleave(SC, 1, 1, 256, 384)
+        for s in (2, 0, 1):
+            quantize(1, 1, EDGES[s], EDGES[s + 1])
+            multiply(1, 1, s)
+            finish(1, s)
         scatter(1)
         nc.sync.dma_start(out=out, in_=window[:])

@@ -55,9 +55,10 @@ def tile_list_hscat_bias_kernel(tc, x, w_words, w_scales, b, wgo, offs, out):
         window = keep.tile([P, T], F32, name="window")
         dummy = keep.tile([P, 1], F32, name="dummy")
 
-        nc.scalar.dma_start(out=w_codes[:], in_=w_words.rearrange("a p n t -> p a (n t)").bitcast(I32))
+        nc.scalar.dma_start(out=w_codes[:, 0, :], in_=w_words[0].rearrange("p n t -> p (n t)").bitcast(I32))
         nc.vector.memset(w_sc[:].rearrange("p a n -> p (a n)").bitcast(I32), 0)
         nc.vector.memset(chunks[:, 1:, 0, 0:HALF:256], 0.0)
+        nc.vector.memset(w_codes[:, 1, 0:1], 0)
         nc.vector.memset(bias[:], 0.0)
         nc.vector.memset(wg[0][:, 0:1], 0.0)
         nc.vector.memset(dummy[:], 0.0)
@@ -69,6 +70,7 @@ def tile_list_hscat_bias_kernel(tc, x, w_words, w_scales, b, wgo, offs, out):
             )
         load_x(0, 1, 0, 256)
         load_x(0, 1, 256, HALF)
+        nc.sync.dma_start(out=w_codes[:, 1, :], in_=w_words[1].rearrange("p n t -> p (n t)").bitcast(I32))
         nc.sync.dma_start(out=bias[:], in_=b.rearrange("(p o) -> p o", o=1))
         nc.sync.dma_start(lists[:], offs)
         nc.sync.dma_start(out=wg[0][:], in_=wgo[:, 0:HALF])
@@ -133,9 +135,11 @@ def tile_list_hscat_bias_kernel(tc, x, w_words, w_scales, b, wgo, offs, out):
         quantize(0, 1, 0, 256)
         multiply(0, 1, 0)
         finish(0, 0)
-        interleave(V, 0, 1, 256, 384)
+        interleave(V, 0, 1, 256, 320)
+        interleave(V, 0, 1, 320, 384)
         interleave(SC, 0, 1, 384, 512)
-        quantize(0, 1, 256, 384)
+        quantize(0, 1, 256, 320)
+        quantize(0, 1, 320, 384)
         multiply(0, 1, 1)
         finish(0, 1)
         quantize(0, 1, 384, 512)
@@ -144,9 +148,11 @@ def tile_list_hscat_bias_kernel(tc, x, w_words, w_scales, b, wgo, offs, out):
         scatter(0)
         interleave(SC, 1, 0, 0, 256)
         interleave(SC, 1, 0, 256, 512)
-        quantize(1, 0, 0, 512)
-        for s in range(3):
-            multiply(1, 0, s)
+        quantize(1, 0, 0, 256)
+        multiply(1, 0, 0)
+        quantize(1, 0, 256, 512)
+        multiply(1, 0, 1)
+        multiply(1, 0, 2)
         interleave(SC, 1, 1, 384, 512)
         interleave(V, 1, 1, 0, 256)
         interleave(SC, 1, 1, 256, 384)

from contextlib import ExitStack

import concourse.mybir as mybir

K, M, T, S = 1024, 128, 2048, 1024
FLOPS = 2 * K * M * S

F32 = mybir.dt.float32
BF16 = mybir.dt.bfloat16
I32 = mybir.dt.int32
U32 = mybir.dt.uint32
U16 = mybir.dt.uint16
U8 = mybir.dt.uint8
FP8X4 = mybir.dt.float8_e4m3fn_x4
IDENT = mybir.ActivationFunctionType.Identity
MULT = mybir.AluOpType.mult

P = 128
J = 4
PASS = P * J
A = K // PASS
HALF = 512
H = S // HALF
EDGES = (0, 256, 384, 512)


def tile_list_hscat_bias_kernel(tc, x, w_words, w_scales, b, wgo, offs, out):
    nc = tc.nc
    with ExitStack() as ctx:
        keep = ctx.enter_context(tc.tile_pool(name="keep", bufs=1))
        psum = ctx.enter_context(tc.psum_pool(name="psum", bufs=1))

        chunks = keep.tile([P, H * A, J, HALF], F32, name="chunks")
        raw, grouped, codes, scales = {}, {}, {}, {}
        for h in range(H):
            for a in range(A):
                raw[h, a] = chunks[:, h * A + a]
                grouped[h, a] = keep.tile([P, HALF, J], BF16, name="grouped%d%d" % (h, a), align_bytes=64)
                codes[h, a] = keep.tile([P, HALF], U32, name="codes%d%d" % (h, a), align_bytes=64)
                scales[h, a] = keep.tile([P, HALF], U8, name="scales%d%d" % (h, a), align_bytes=64)

        def load_x(h, a, c0=0, c1=HALF):
            nc.sync.dma_start(
                out=raw[h, a][:, :, c0:c1],
                in_=x[a * PASS:(a + 1) * PASS, h * HALF + c0:h * HALF + c1].rearrange("(p j) w -> p j w", j=J),
            )

        w_codes = keep.tile([P, A, M], I32, name="w_codes", align_bytes=64)
        w_sc = keep.tile([P, A, M], U8, name="w_sc", align_bytes=64)
        bias = keep.tile([P, 1], F32, name="bias")
        lists = keep.tile([P, S // 16], U16, name="lists")
        wg = {}
        for h in range(H):
            wg[h] = keep.tile([P, HALF], F32, name="wg%d" % h)
        window = keep.tile([P, T], F32, name="window")
        dummy = keep.tile([P, 1], F32, name="dummy")

        nc.scalar.dma_start(out=w_codes[:, 0, :], in_=w_words[0].rearrange("p n t -> p (n t)").bitcast(I32))
        nc.vector.memset(w_sc[:].rearrange("p a n -> p (a n)").bitcast(I32), 0)
        nc.vector.memset(chunks[:, 1:, 0, 0:HALF:256], 0.0)
        nc.vector.memset(w_codes[:, 1, 0:1], 0)
        nc.vector.memset(bias[:], 0.0)
        nc.vector.memset(wg[0][:, 0:1], 0.0)
        nc.vector.memset(dummy[:], 0.0)
        load_x(0, 0)
        for q in range(4):
            nc.sync.dma_start(
                out=w_sc[32 * q:32 * q + 4, :, :].bitcast(I32),
                in_=w_scales[:, 4 * q:4 * q + 4, :].rearrange("a r n -> r a n").bitcast(I32),
            )
        load_x(0, 1, 0, 256)
        load_x(0, 1, 256, HALF)
        nc.sync.dma_start(out=w_codes[:, 1, :], in_=w_words[1].rearrange("p n t -> p (n t)").bitcast(I32))
        nc.sync.dma_start(out=bias[:], in_=b.rearrange("(p o) -> p o", o=1))
        nc.sync.dma_start(lists[:], offs)
        nc.sync.dma_start(out=wg[0][:], in_=wgo[:, 0:HALF])
        load_x(1, 0)
        load_x(1, 1)
        nc.sync.dma_start(out=wg[1][:], in_=wgo[:, HALF:S])
        nc.scalar.activation(dummy[:], dummy[:], IDENT)
        nc.vector.memset(window[:], 0.0)

        y, acc = {}, {}
        for h in range(H):
            y[h] = keep.tile([M, HALF], F32, name="y%d" % h)
            for s in range(3):
                acc[h, s] = psum.tile([M, EDGES[s + 1] - EDGES[s]], F32, name="acc%d%d" % (h, s))

        def interleave(copy, h, a, c0, c1):
            copy(
                grouped[h, a][:, c0:c1, :].rearrange("p (c i) t -> p c t i", i=4),
                raw[h, a][:, :, c0:c1].rearrange("p t (c i) -> p c t i", i=4),
            )

        def quantize(h, a, c0, c1):
            nc.vector.quantize_mx(
                out=codes[h, a][:, c0:c1].bitcast(FP8X4),
                scales=scales[h, a][:, c0:c1],
                in_=grouped[h, a][:, c0:c1, :].rearrange("p w j -> p (w j)"),
            )

        def multiply(h, a, s):
            c0, c1 = EDGES[s:s + 2]
            nc.tensor.matmul_mx(
                out=acc[h, s][:],
                lhsT=w_codes[:, a, :].bitcast(FP8X4),
                lhsT_scale=w_sc[:, a, :],
                rhs=codes[h, a][:, c0:c1].bitcast(FP8X4),
                rhs_scale=scales[h, a][:, c0:c1],
                start=(a == 0),
                stop=(a == A - 1),
            )

        def finish(h, s):
            c0, c1 = EDGES[s:s + 2]
            nc.scalar.activation(y[h][:, c0:c1], acc[h, s][:], IDENT, bias=bias[:])

        def scatter(h):
            nc.vector.tensor_tensor(
                window[:].indirect(lists[:, h * HALF // 16:(h + 1) * HALF // 16]),
                y[h][:],
                wg[h][:],
                MULT,
            )

        V, SC = nc.vector.tensor_copy, nc.scalar.copy
        interleave(V, 0, 0, 0, 128)
        interleave(V, 0, 0, 128, 256)
        interleave(SC, 0, 0, 256, 512)
        quantize(0, 0, 0, 512)
        for s in range(3):
            multiply(0, 0, s)
        interleave(V, 0, 1, 0, 160)
        interleave(SC, 0, 1, 160, 256)
        quantize(0, 1, 0, 256)
        multiply(0, 1, 0)
        finish(0, 0)
        interleave(V, 0, 1, 256, 320)
        interleave(V, 0, 1, 320, 384)
        interleave(SC, 0, 1, 384, 512)
        quantize(0, 1, 256, 320)
        quantize(0, 1, 320, 384)
        multiply(0, 1, 1)
        finish(0, 1)
        quantize(0, 1, 384, 512)
        multiply(0, 1, 2)
        finish(0, 2)
        scatter(0)
        interleave(SC, 1, 0, 0, 256)
        interleave(SC, 1, 0, 256, 512)
        quantize(1, 0, 0, 256)
        multiply(1, 0, 0)
        quantize(1, 0, 256, 512)
        multiply(1, 0, 1)
        multiply(1, 0, 2)
        interleave(SC, 1, 1, 384, 512)
        interleave(V, 1, 1, 0, 256)
        interleave(SC, 1, 1, 256, 384)
        for s in (2, 0, 1):
            quantize(1, 1, EDGES[s], EDGES[s + 1])
            multiply(1, 1, s)
            finish(1, s)
        scatter(1)
        nc.sync.dma_start(out=out, in_=window[:])
